import numpy as np
import ml_dtypes


def mxq(x, axis, fmt="e4m3"):
    dtype, down = {"e4m3": (ml_dtypes.float8_e4m3fn, 7), "e5m2": (ml_dtypes.float8_e5m2, 14)}[fmt]
    v = np.moveaxis(np.asarray(x, np.float32).astype(ml_dtypes.bfloat16).astype(np.float64), axis, -1)
    blocks = v.reshape(v.shape[:-1] + (-1, 32))
    amax = np.abs(blocks).max(-1, keepdims=True)
    byte = np.maximum(np.where(amax > 0, np.frexp(amax)[1] - 1 + 127, 0) - down, 1)
    scale = np.exp2(byte - 127.0)
    codes = (blocks / scale).astype(np.float32).astype(dtype).astype(np.float64)
    return np.moveaxis((codes * scale).reshape(v.shape), -1, axis)


WIDE = False


def mx_kscale(k):
    if not WIDE:
        return np.ones(k)
    levels = np.array([10, -10, 5, -5, 0])
    if k % 512:
        return np.exp2(np.random.permutation(np.resize(levels, k // 32))).repeat(32)
    a = np.empty((k // 512, 16))
    for p in range(k // 512):
        a[p, :8] = np.random.permutation(np.resize(levels, 8))
        for g in range(8):
            far = levels[np.abs(levels - a[p, g]) >= 10]
            a[p, g + 8] = far[np.random.randint(len(far))]
    return np.exp2(a.ravel()).repeat(32)


def f64(x):
    return np.asarray(x).astype(np.float64)


def striped(idx):
    return np.tile(idx.reshape(-1, 16).T, (8, 1)).astype(np.uint16)


def unstriped(offs):
    return offs[:16].T.reshape(-1).astype(np.int64)


def relu(v):
    return np.maximum(v, 0.0)


K, T, E, C, N = 1536, 512, 4, 256, 128


def by_expert(wq, xq):
    return np.concatenate([wq[e].T @ xq[:, e * C:(e + 1) * C] for e in range(E)], axis=1)


def setup_inputs():
    n = np.random.standard_normal
    s = mx_kscale(K)[:, None]
    first = np.random.permutation(np.repeat(np.arange(E), T // E))
    second = (first + 1 + np.random.permutation(np.repeat(np.arange(E - 1), -(-T // (E - 1)))[:T])) % E
    while np.bincount(second, minlength=E).max() != T // E:
        load = np.bincount(second, minlength=E); hi, lo = int(load.argmax()), int(load.argmin())
        t = np.flatnonzero((second == hi) & (first != lo))[0]; second[t] = lo
    slot_token = np.empty(E * C, np.int64); pos = np.empty((2, T), np.int64); fill = np.zeros(E, np.int64)
    place = np.stack([np.random.permutation(C) for _ in range(E)])
    for r, deal in enumerate((first, second)):
        for t in np.random.permutation(T):
            e = deal[t]; j = e * C + place[e, fill[e]]; fill[e] += 1; slot_token[j] = t; pos[r, t] = j
    g = np.random.uniform(0.2, 0.8, T)
    return {
        "xT": (n((K, T)) * s).astype(np.float32),
        "w": (n((E, K, N)) / np.sqrt(K) / s[None]).astype(np.float32),
        "b": (0.3 * n((N, E))).astype(np.float32),
        "gate": np.stack([np.tile(g, (N, 1)), np.tile(1.0 - g, (N, 1))]).astype(np.float32),
        "offs": striped(slot_token),
        "pos1": striped(pos[0]),
        "pos2": striped(pos[1]),
    }


def reference(xT, w, b, gate, offs, pos1, pos2):
    idx = unstriped(offs)
    xq = mxq(f64(xT)[:, idx], 0, "e4m3")
    y = by_expert(mxq(f64(w), 1, "e4m3"), xq)
    y = relu(y + np.repeat(f64(b), C, axis=1))
    return f64(gate[0]) * y[:, unstriped(pos1)] + f64(gate[1]) * y[:, unstriped(pos2)]

@@ -1,0 +1,143 @@
+from contextlib import ExitStack
+
+import concourse.mybir as mybir
+
+K, T, E, C, N = 1536, 512, 4, 256, 128
+FLOPS = 2 * K * N * E * C
+
+F32 = mybir.dt.float32
+BF16 = mybir.dt.bfloat16
+I32 = mybir.dt.int32
+U32 = mybir.dt.uint32
+U16 = mybir.dt.uint16
+U8 = mybir.dt.uint8
+FP8X4 = mybir.dt.float8_e4m3fn_x4
+MULT = mybir.AluOpType.mult
+RELU = mybir.ActivationFunctionType.Relu
+
+P = 128
+PACK = 4
+A = K // (P * PACK)
+WIN = 1408
+W_GROUPS = (4, 4, 2, 1, 1)
+
+
+def tile_routed_moe_kernel(tc, xT, w, b, gate, offs, pos1, pos2, out):
+    nc = tc.nc
+    with ExitStack() as ctx:
+        keep = ctx.enter_context(tc.tile_pool(name="keep", bufs=1))
+        psum = ctx.enter_context(tc.psum_pool(name="psum", bufs=1))
+
+        offs_t = keep.tile([P, E * C // 16], U16, name="offs_t")
+        pos1_t = keep.tile([P, T // 16], U16, name="pos1_t")
+        pos2_t = keep.tile([P, T // 16], U16, name="pos2_t")
+        bias = keep.tile([P, E], F32, name="bias")
+        gates = keep.tile([P, 2, T], F32, name="gates")
+
+        x_raw = [keep.tile([P, PACK, T], F32, name=f"x_raw{a}") for a in range(A)]
+        x_grp = [keep.tile([P, T, PACK], BF16, name=f"x_grp{a}", align_bytes=64) for a in range(A)]
+        x_codes = [keep.tile([P, WIN], I32, name=f"x_codes{a}", align_bytes=64) for a in range(A)]
+        x_scales = keep.tile([P, WIN], U8, name="x_scales", align_bytes=64)
+        s_codes = [keep.tile([P, E * C], U32, name=f"s_codes{a}", align_bytes=64) for a in range(A)]
+        s_scales = keep.tile([P, E * C], U8, name="s_scales", align_bytes=64)
+
+        w_raw, w_grp, w_codes, w_scales = [], [], [], []
+        for g, n in enumerate(W_GROUPS):
+            w_raw.append(keep.tile([P, n, PACK, N], F32, name=f"w_raw{g}"))
+            w_grp.append(keep.tile([P, n, N, PACK], BF16, name=f"w_grp{g}", align_bytes=64))
+            w_codes.append(keep.tile([P, n, N], U32, name=f"w_codes{g}", align_bytes=64))
+            w_scales.append(keep.tile([P, n, N], U8, name=f"w_scales{g}", align_bytes=64))
+
+        y = keep.tile([P, E * C], F32, name="y")
+        t1 = keep.tile([P, T], F32, name="t1")
+        t2 = keep.tile([P, T], F32, name="t2")
+        res = keep.tile([P, T], F32, name="res")
+
+        xv = xT.rearrange("(a p j) t -> a p j t", p=P, j=PACK)
+        H = T // 2
+        for a in range(A):
+            for h in range(2):
+                nc.sync.dma_start(out=x_raw[a][:, :, h * H:(h + 1) * H], in_=xv[a, :, :, h * H:(h + 1) * H])
+            if a == 0:
+                nc.sync.dma_start(offs_t[:], offs)
+        wv = w.rearrange("e (a p j) n -> p (e a) j n", p=P, j=PACK)
+        start = 0
+        for g, n in enumerate(W_GROUPS):
+            nc.sync.dma_start(out=w_raw[g][:], in_=wv[:, start:start + n, :, :])
+            start += n
+            if g == 0:
+                nc.sync.dma_start(out=bias[:], in_=b)
+        nc.sync.dma_start(pos1_t[:], pos1)
+        nc.sync.dma_start(pos2_t[:], pos2)
+        nc.sync.dma_start(out=gates[:], in_=gate.rearrange("g p t -> p g t"))
+
+        nc.gpsimd.memset(x_scales[:], 0)
+        for a in range(A):
+            nc.vector.memset(x_codes[a][:, T:], 0)
+
+        def group_x(copy, a, t0, n):
+            copy(
+                out=x_grp[a][:, t0:t0 + n, :].rearrange("p (c i) j -> p c j i", i=4),
+                in_=x_raw[a][:, :, t0:t0 + n].rearrange("p j (c i) -> p c j i", i=4),
+            )
+
+        def quant_x(a, t0, n):
+            nc.vector.quantize_mx(
+                out=x_codes[a][:, t0:t0 + n].bitcast(FP8X4),
+                scales=x_scales[4 * a:, t0:t0 + n],
+                in_=x_grp[a][:, t0:t0 + n, :].rearrange("p t j -> p (t j)"),
+            )
+
+        def gather_x(a):
+            nc.vector.tensor_copy(s_codes[a][:], x_codes[a][:].bitcast(U32).indirect(offs_t[:]))
+
+        group_x(nc.vector.tensor_copy, 0, 0, H)
+        quant_x(0, 0, H)
+        group_x(nc.vector.tensor_copy, 0, H, H)
+        quant_x(0, H, H)
+        gather_x(0)
+        group_x(nc.scalar.copy, 1, 0, H)
+        group_x(nc.scalar.copy, 1, H, H)
+        quant_x(1, 0, T)
+        gather_x(1)
+        group_x(nc.scalar.copy, 2, 0, H)
+        group_x(nc.scalar.copy, 2, H, H)
+        quant_x(2, 0, T)
+        gather_x(2)
+        nc.vector.tensor_copy(s_scales[:], x_scales[:].indirect(offs_t[:]))
+
+        where = []
+        for g, n in enumerate(W_GROUPS):
+            nc.scalar.copy(
+                out=w_grp[g][:].rearrange("p b (c i) j -> p b c j i", i=4),
+                in_=w_raw[g][:].rearrange("p b j (c i) -> p b c j i", i=4),
+            )
+            nc.vector.quantize_mx(
+                out=w_codes[g][:].rearrange("p b n -> p (b n)").bitcast(FP8X4),
+                scales=w_scales[g][:].rearrange("p b n -> p (b n)"),
+                in_=w_grp[g][:].rearrange("p b n j -> p (b n j)"),
+            )
+            where += [(g, i) for i in range(n)]
+
+        for e in range(E):
+            acc = psum.tile([N, C], F32, name=f"acc{e}")
+            cols = slice(e * C, (e + 1) * C)
+            for a in range(A):
+                g, i = where[e * A + a]
+                nc.tensor.matmul_mx(
+                    out=acc[:],
+                    lhsT=w_codes[g][:, i, :].bitcast(FP8X4),
+                    lhsT_scale=w_scales[g][:, i, :],
+                    rhs=s_codes[a][:, cols].bitcast(FP8X4),
+                    rhs_scale=s_scales[4 * a:, cols],
+                    start=(a == 0),
+                    stop=(a == A - 1),
+                )
+            nc.scalar.activation(out=y[:, cols], in_=acc[:], func=RELU, bias=bias[:, e:e + 1])
+
+        nc.vector.tensor_tensor(t1[:], y[:].indirect(pos1_t[:]), gates[:, 0, :], MULT)
+        nc.vector.tensor_tensor(t2[:], y[:].indirect(pos2_t[:]), gates[:, 1, :], MULT)
+        for h in range(2):
+            cols = slice(h * H, (h + 1) * H)
+            nc.vector.tensor_add(res[:, cols], t1[:, cols], t2[:, cols])
+            nc.sync.dma_start(out=out[:, cols], in_=res[:, cols])

@@ -13,13 +13,15 @@ U16 = mybir.dt.uint16
 U8 = mybir.dt.uint8
 FP8X4 = mybir.dt.float8_e4m3fn_x4
 MULT = mybir.AluOpType.mult
+ADD = mybir.AluOpType.add
 RELU = mybir.ActivationFunctionType.Relu
 
 P = 128
 PACK = 4
 A = K // (P * PACK)
 WIN = 1408
-W_GROUPS = (4, 4, 2, 1, 1)
+VECTOR_RELU = (2,)
+MAX = mybir.AluOpType.max
 
 
 def tile_routed_moe_kernel(tc, xT, w, b, gate, offs, pos1, pos2, out):
@@ -38,106 +40,138 @@ def tile_routed_moe_kernel(tc, xT, w, b, gate, offs, pos1, pos2, out):
         x_grp = [keep.tile([P, T, PACK], BF16, name=f"x_grp{a}", align_bytes=64) for a in range(A)]
         x_codes = [keep.tile([P, WIN], I32, name=f"x_codes{a}", align_bytes=64) for a in range(A)]
         x_scales = keep.tile([P, WIN], U8, name="x_scales", align_bytes=64)
-        s_codes = [keep.tile([P, E * C], U32, name=f"s_codes{a}", align_bytes=64) for a in range(A)]
+        s_codes = [keep.tile([P, E * C], U32, name=f"s_codes{a}", align_bytes=64) for a in range(A - 1)]
         s_scales = keep.tile([P, E * C], U8, name="s_scales", align_bytes=64)
 
-        w_raw, w_grp, w_codes, w_scales = [], [], [], []
-        for g, n in enumerate(W_GROUPS):
-            w_raw.append(keep.tile([P, n, PACK, N], F32, name=f"w_raw{g}"))
-            w_grp.append(keep.tile([P, n, N, PACK], BF16, name=f"w_grp{g}", align_bytes=64))
-            w_codes.append(keep.tile([P, n, N], U32, name=f"w_codes{g}", align_bytes=64))
-            w_scales.append(keep.tile([P, n, N], U8, name=f"w_scales{g}", align_bytes=64))
+        w_raw = [keep.tile([P, E, PACK, N], F32, name=f"w_raw{a}") for a in range(A)]
+        w_codes = [keep.tile([P, E, N], U32, name=f"w_codes{a}", align_bytes=64) for a in range(A)]
+        w_scales = [keep.tile([P, E, N], U8, name=f"w_scales{a}", align_bytes=64) for a in range(A)]
 
         y = keep.tile([P, E * C], F32, name="y")
         t1 = keep.tile([P, T], F32, name="t1")
         t2 = keep.tile([P, T], F32, name="t2")
         res = keep.tile([P, T], F32, name="res")
+        acc = [psum.tile([N, C], F32, name=f"acc{e}") for e in range(E)]
 
         xv = xT.rearrange("(a p j) t -> a p j t", p=P, j=PACK)
-        H = T // 2
-        for a in range(A):
-            for h in range(2):
-                nc.sync.dma_start(out=x_raw[a][:, :, h * H:(h + 1) * H], in_=xv[a, :, :, h * H:(h + 1) * H])
+        wv = w.rearrange("e (a p j) n -> a p e j n", p=P, j=PACK)
+        for a, cuts in enumerate((((0, 256), (256, 512)),) * 3):
+            for c0, c1 in cuts:
+                nc.sync.dma_start(out=x_raw[a][:, :, c0:c1], in_=xv[a, :, :, c0:c1])
             if a == 0:
                 nc.sync.dma_start(offs_t[:], offs)
-        wv = w.rearrange("e (a p j) n -> p (e a) j n", p=P, j=PACK)
-        start = 0
-        for g, n in enumerate(W_GROUPS):
-            nc.sync.dma_start(out=w_raw[g][:], in_=wv[:, start:start + n, :, :])
-            start += n
-            if g == 0:
+        for a in range(A):
+            for e0, e1 in ((0, 2), (2, 4)):
+                nc.sync.dma_start(out=w_raw[a][:, e0:e1], in_=wv[a, :, e0:e1])
+            if a == 0:
                 nc.sync.dma_start(out=bias[:], in_=b)
         nc.sync.dma_start(pos1_t[:], pos1)
         nc.sync.dma_start(pos2_t[:], pos2)
         nc.sync.dma_start(out=gates[:], in_=gate.rearrange("g p t -> p g t"))
 
         nc.gpsimd.memset(x_scales[:], 0)
-        for a in range(A):
-            nc.vector.memset(x_codes[a][:, T:], 0)
 
-        def group_x(copy, a, t0, n):
+        def group_x(copy, a, t0, t1_):
             copy(
-                out=x_grp[a][:, t0:t0 + n, :].rearrange("p (c i) j -> p c j i", i=4),
-                in_=x_raw[a][:, :, t0:t0 + n].rearrange("p j (c i) -> p c j i", i=4),
+                out=x_grp[a][:, t0:t1_, :].rearrange("p (c i) j -> p c j i", i=4),
+                in_=x_raw[a][:, :, t0:t1_].rearrange("p j (c i) -> p c j i", i=4),
             )
 
-        def quant_x(a, t0, n):
+        def quant_x(a, t0, t1_):
             nc.vector.quantize_mx(
-                out=x_codes[a][:, t0:t0 + n].bitcast(FP8X4),
-                scales=x_scales[4 * a:, t0:t0 + n],
-                in_=x_grp[a][:, t0:t0 + n, :].rearrange("p t j -> p (t j)"),
+                out=x_codes[a][:, t0:t1_].bitcast(FP8X4),
+                scales=x_scales[4 * a:, t0:t1_],
+                in_=x_grp[a][:, t0:t1_, :].rearrange("p t j -> p (t j)"),
             )
 
-        def gather_x(a):
-            nc.vector.tensor_copy(s_codes[a][:], x_codes[a][:].bitcast(U32).indirect(offs_t[:]))
+        def gather_x(dst, a, s0, s1):
+            nc.vector.tensor_copy(dst, x_codes[a][:].bitcast(U32).indirect(offs_t[:, s0 // 16:s1 // 16]))
 
-        group_x(nc.vector.tensor_copy, 0, 0, H)
-        quant_x(0, 0, H)
-        group_x(nc.vector.tensor_copy, 0, H, H)
-        quant_x(0, H, H)
-        gather_x(0)
-        group_x(nc.scalar.copy, 1, 0, H)
-        group_x(nc.scalar.copy, 1, H, H)
-        quant_x(1, 0, T)
-        gather_x(1)
-        group_x(nc.scalar.copy, 2, 0, H)
-        group_x(nc.scalar.copy, 2, H, H)
-        quant_x(2, 0, T)
-        gather_x(2)
-        nc.vector.tensor_copy(s_scales[:], x_scales[:].indirect(offs_t[:]))
+        def gather_s(s0, s1):
+            nc.vector.tensor_copy(s_scales[:, s0:s1], x_scales[:].indirect(offs_t[:, s0 // 16:s1 // 16]))
 
-        where = []
-        for g, n in enumerate(W_GROUPS):
+        def group_w(grp, a, e0, e1):
             nc.scalar.copy(
-                out=w_grp[g][:].rearrange("p b (c i) j -> p b c j i", i=4),
-                in_=w_raw[g][:].rearrange("p b j (c i) -> p b c j i", i=4),
+                out=grp[:, e0:e1].rearrange("p b (c i) j -> p b c j i", i=4),
+                in_=w_raw[a][:, e0:e1].rearrange("p b j (c i) -> p b c j i", i=4),
             )
-            nc.vector.quantize_mx(
-                out=w_codes[g][:].rearrange("p b n -> p (b n)").bitcast(FP8X4),
-                scales=w_scales[g][:].rearrange("p b n -> p (b n)"),
-                in_=w_grp[g][:].rearrange("p b n j -> p (b n j)"),
-            )
-            where += [(g, i) for i in range(n)]
 
-        for e in range(E):
-            acc = psum.tile([N, C], F32, name=f"acc{e}")
+        def quant_w(grp, a, e0, e1):
+            nc.vector.quantize_mx(
+                out=w_codes[a][:, e0:e1].rearrange("p b n -> p (b n)").bitcast(FP8X4),
+                scales=w_scales[a][:, e0:e1].rearrange("p b n -> p (b n)"),
+                in_=grp[:, e0:e1].rearrange("p b n j -> p (b n j)"),
+            )
+
+        def multiply(a, e, slots):
             cols = slice(e * C, (e + 1) * C)
-            for a in range(A):
-                g, i = where[e * A + a]
-                nc.tensor.matmul_mx(
-                    out=acc[:],
-                    lhsT=w_codes[g][:, i, :].bitcast(FP8X4),
-                    lhsT_scale=w_scales[g][:, i, :],
-                    rhs=s_codes[a][:, cols].bitcast(FP8X4),
-                    rhs_scale=s_scales[4 * a:, cols],
-                    start=(a == 0),
-                    stop=(a == A - 1),
-                )
-            nc.scalar.activation(out=y[:, cols], in_=acc[:], func=RELU, bias=bias[:, e:e + 1])
+            nc.tensor.matmul_mx(
+                out=acc[e][:],
+                lhsT=w_codes[a][:, e, :].bitcast(FP8X4),
+                lhsT_scale=w_scales[a][:, e, :],
+                rhs=slots.bitcast(FP8X4),
+                rhs_scale=s_scales[4 * a:, cols],
+                start=(a == 0),
+                stop=(a == A - 1),
+            )
+            if a == A - 1:
+                if e in VECTOR_RELU:
+                    nc.vector.tensor_scalar(y[:, cols], acc[e][:], bias[:, e:e + 1], 0.0, ADD, MAX)
+                else:
+                    nc.scalar.activation(out=y[:, cols], in_=acc[e][:], func=RELU, bias=bias[:, e:e + 1])
+
+        V, S = nc.vector.tensor_copy, nc.scalar.copy
+        group_x(V, 0, 0, 256)
+        quant_x(0, 0, 256)
+        group_x(S, 0, 416, 512)
+        group_x(V, 0, 256, 416)
+        quant_x(0, 256, 512)
+        gather_x(s_codes[0][:, :832], 0, 0, 832)
+        group_x(S, 1, 0, 256)
+        group_x(S, 1, 256, 512)
+        quant_x(1, 0, 512)
+        gather_x(s_codes[0][:, 832:], 0, 832, 1024)
+        gather_x(s_codes[1][:, :832], 1, 0, 832)
+        group_x(S, 2, 0, 256)
+        group_x(S, 2, 256, 512)
+        quant_x(2, 0, 512)
+        gather_x(s_codes[1][:, 832:], 1, 832, 1024)
+        gather_s(0, 1024)
+
+        w_grp0 = keep.tile([P, E, N, PACK], BF16, name="w_grp0", tag="swap0", align_bytes=64)
+        group_w(w_grp0, 0, 0, 2)
+        group_w(w_grp0, 0, 2, 4)
+        quant_w(w_grp0, 0, 0, 4)
+        for e in range(E):
+            multiply(0, e, s_codes[0][:, e * C:(e + 1) * C])
+
+        late0 = keep.tile([P, E * C // 2], U32, name="late0", tag="swap0", align_bytes=64)
+        gather_x(late0[:], 2, 0, 512)
+        w_grp1 = keep.tile([P, E, N, PACK], BF16, name="w_grp1", tag="swap1", align_bytes=64)
+        group_w(w_grp1, 1, 0, 2)
+        group_w(w_grp1, 1, 2, 4)
+        quant_w(w_grp1, 1, 0, 4)
+        for e in range(E):
+            multiply(1, e, s_codes[1][:, e * C:(e + 1) * C])
+        w_grp2 = keep.tile([P, E, N, PACK], BF16, name="w_grp2", align_bytes=64)
+        group_w(w_grp2, 2, 0, 2)
+        quant_w(w_grp2, 2, 0, 2)
+        for e in range(2):
+            multiply(2, e, late0[:, e * C:(e + 1) * C])
+        late1 = keep.tile([P, E * C // 2], U32, name="late1", tag="swap1", align_bytes=64)
+        gather_x(late1[:], 2, 512, 1024)
+        group_w(w_grp2, 2, 2, 4)
+        quant_w(w_grp2, 2, 2, 4)
+        for e in range(2, E):
+            multiply(2, e, late1[:, (e - 2) * C:(e - 1) * C])
 
         nc.vector.tensor_tensor(t1[:], y[:].indirect(pos1_t[:]), gates[:, 0, :], MULT)
-        nc.vector.tensor_tensor(t2[:], y[:].indirect(pos2_t[:]), gates[:, 1, :], MULT)
-        for h in range(2):
-            cols = slice(h * H, (h + 1) * H)
+        for c0 in range(0, T, T // 2):
+            cols = slice(c0, c0 + T // 2)
+            nc.vector.tensor_tensor(
+                t2[:, cols], y[:].indirect(pos2_t[:, c0 // 16:(c0 + T // 2) // 16]), gates[:, 1, cols], MULT
+            )
+        for c0 in range(0, T, T // 2):
+            cols = slice(c0, c0 + T // 2)
             nc.vector.tensor_add(res[:, cols], t1[:, cols], t2[:, cols])
             nc.sync.dma_start(out=out[:, cols], in_=res[:, cols])

from contextlib import ExitStack

import concourse.mybir as mybir

K, T, E, C, N = 1536, 512, 4, 256, 128
FLOPS = 2 * K * N * E * C

F32 = mybir.dt.float32
BF16 = mybir.dt.bfloat16
I32 = mybir.dt.int32
U32 = mybir.dt.uint32
U16 = mybir.dt.uint16
U8 = mybir.dt.uint8
FP8X4 = mybir.dt.float8_e4m3fn_x4
MULT = mybir.AluOpType.mult
ADD = mybir.AluOpType.add
RELU = mybir.ActivationFunctionType.Relu

P = 128
PACK = 4
A = K // (P * PACK)
WIN = 1408
VECTOR_RELU = (2,)
MAX = mybir.AluOpType.max


def tile_routed_moe_kernel(tc, xT, w, b, gate, offs, pos1, pos2, out):
    nc = tc.nc
    with ExitStack() as ctx:
        keep = ctx.enter_context(tc.tile_pool(name="keep", bufs=1))
        psum = ctx.enter_context(tc.psum_pool(name="psum", bufs=1))

        offs_t = keep.tile([P, E * C // 16], U16, name="offs_t")
        pos1_t = keep.tile([P, T // 16], U16, name="pos1_t")
        pos2_t = keep.tile([P, T // 16], U16, name="pos2_t")
        bias = keep.tile([P, E], F32, name="bias")
        gates = keep.tile([P, 2, T], F32, name="gates")

        x_raw = [keep.tile([P, PACK, T], F32, name=f"x_raw{a}") for a in range(A)]
        x_grp = [keep.tile([P, T, PACK], BF16, name=f"x_grp{a}", align_bytes=64) for a in range(A)]
        x_codes = [keep.tile([P, WIN], I32, name=f"x_codes{a}", align_bytes=64) for a in range(A)]
        x_scales = keep.tile([P, WIN], U8, name="x_scales", align_bytes=64)
        s_codes = [keep.tile([P, E * C], U32, name=f"s_codes{a}", align_bytes=64) for a in range(A - 1)]
        s_scales = keep.tile([P, E * C], U8, name="s_scales", align_bytes=64)

        w_raw = [keep.tile([P, E, PACK, N], F32, name=f"w_raw{a}") for a in range(A)]
        w_codes = [keep.tile([P, E, N], U32, name=f"w_codes{a}", align_bytes=64) for a in range(A)]
        w_scales = [keep.tile([P, E, N], U8, name=f"w_scales{a}", align_bytes=64) for a in range(A)]

        y = keep.tile([P, E * C], F32, name="y")
        t1 = keep.tile([P, T], F32, name="t1")
        t2 = keep.tile([P, T], F32, name="t2")
        res = keep.tile([P, T], F32, name="res")
        acc = [psum.tile([N, C], F32, name=f"acc{e}") for e in range(E)]

        xv = xT.rearrange("(a p j) t -> a p j t", p=P, j=PACK)
        wv = w.rearrange("e (a p j) n -> a p e j n", p=P, j=PACK)
        for a, cuts in enumerate((((0, 256), (256, 512)),) * 3):
            for c0, c1 in cuts:
                nc.sync.dma_start(out=x_raw[a][:, :, c0:c1], in_=xv[a, :, :, c0:c1])
            if a == 0:
                nc.sync.dma_start(offs_t[:], offs)
        for a in range(A):
            for e0, e1 in ((0, 2), (2, 4)):
                nc.sync.dma_start(out=w_raw[a][:, e0:e1], in_=wv[a, :, e0:e1])
            if a == 0:
                nc.sync.dma_start(out=bias[:], in_=b)
        nc.sync.dma_start(pos1_t[:], pos1)
        nc.sync.dma_start(pos2_t[:], pos2)
        nc.sync.dma_start(out=gates[:], in_=gate.rearrange("g p t -> p g t"))

        nc.gpsimd.memset(x_scales[:], 0)

        def group_x(copy, a, t0, t1_):
            copy(
                out=x_grp[a][:, t0:t1_, :].rearrange("p (c i) j -> p c j i", i=4),
                in_=x_raw[a][:, :, t0:t1_].rearrange("p j (c i) -> p c j i", i=4),
            )

        def quant_x(a, t0, t1_):
            nc.vector.quantize_mx(
                out=x_codes[a][:, t0:t1_].bitcast(FP8X4),
                scales=x_scales[4 * a:, t0:t1_],
                in_=x_grp[a][:, t0:t1_, :].rearrange("p t j -> p (t j)"),
            )

        def gather_x(dst, a, s0, s1):
            nc.vector.tensor_copy(dst, x_codes[a][:].bitcast(U32).indirect(offs_t[:, s0 // 16:s1 // 16]))

        def gather_s(s0, s1):
            nc.vector.tensor_copy(s_scales[:, s0:s1], x_scales[:].indirect(offs_t[:, s0 // 16:s1 // 16]))

        def group_w(grp, a, e0, e1):
            nc.scalar.copy(
                out=grp[:, e0:e1].rearrange("p b (c i) j -> p b c j i", i=4),
                in_=w_raw[a][:, e0:e1].rearrange("p b j (c i) -> p b c j i", i=4),
            )

        def quant_w(grp, a, e0, e1):
            nc.vector.quantize_mx(
                out=w_codes[a][:, e0:e1].rearrange("p b n -> p (b n)").bitcast(FP8X4),
                scales=w_scales[a][:, e0:e1].rearrange("p b n -> p (b n)"),
                in_=grp[:, e0:e1].rearrange("p b n j -> p (b n j)"),
            )

        def multiply(a, e, slots):
            cols = slice(e * C, (e + 1) * C)
            nc.tensor.matmul_mx(
                out=acc[e][:],
                lhsT=w_codes[a][:, e, :].bitcast(FP8X4),
                lhsT_scale=w_scales[a][:, e, :],
                rhs=slots.bitcast(FP8X4),
                rhs_scale=s_scales[4 * a:, cols],
                start=(a == 0),
                stop=(a == A - 1),
            )
            if a == A - 1:
                if e in VECTOR_RELU:
                    nc.vector.tensor_scalar(y[:, cols], acc[e][:], bias[:, e:e + 1], 0.0, ADD, MAX)
                else:
                    nc.scalar.activation(out=y[:, cols], in_=acc[e][:], func=RELU, bias=bias[:, e:e + 1])

        V, S = nc.vector.tensor_copy, nc.scalar.copy
        group_x(V, 0, 0, 256)
        quant_x(0, 0, 256)
        group_x(S, 0, 416, 512)
        group_x(V, 0, 256, 416)
        quant_x(0, 256, 512)
        gather_x(s_codes[0][:, :832], 0, 0, 832)
        group_x(S, 1, 0, 256)
        group_x(S, 1, 256, 512)
        quant_x(1, 0, 512)
        gather_x(s_codes[0][:, 832:], 0, 832, 1024)
        gather_x(s_codes[1][:, :832], 1, 0, 832)
        group_x(S, 2, 0, 256)
        group_x(S, 2, 256, 512)
        quant_x(2, 0, 512)
        gather_x(s_codes[1][:, 832:], 1, 832, 1024)
        gather_s(0, 1024)

        w_grp0 = keep.tile([P, E, N, PACK], BF16, name="w_grp0", tag="swap0", align_bytes=64)
        group_w(w_grp0, 0, 0, 2)
        group_w(w_grp0, 0, 2, 4)
        quant_w(w_grp0, 0, 0, 4)
        for e in range(E):
            multiply(0, e, s_codes[0][:, e * C:(e + 1) * C])

        late0 = keep.tile([P, E * C // 2], U32, name="late0", tag="swap0", align_bytes=64)
        gather_x(late0[:], 2, 0, 512)
        w_grp1 = keep.tile([P, E, N, PACK], BF16, name="w_grp1", tag="swap1", align_bytes=64)
        group_w(w_grp1, 1, 0, 2)
        group_w(w_grp1, 1, 2, 4)
        quant_w(w_grp1, 1, 0, 4)
        for e in range(E):
            multiply(1, e, s_codes[1][:, e * C:(e + 1) * C])
        w_grp2 = keep.tile([P, E, N, PACK], BF16, name="w_grp2", align_bytes=64)
        group_w(w_grp2, 2, 0, 2)
        quant_w(w_grp2, 2, 0, 2)
        for e in range(2):
            multiply(2, e, late0[:, e * C:(e + 1) * C])
        late1 = keep.tile([P, E * C // 2], U32, name="late1", tag="swap1", align_bytes=64)
        gather_x(late1[:], 2, 512, 1024)
        group_w(w_grp2, 2, 2, 4)
        quant_w(w_grp2, 2, 2, 4)
        for e in range(2, E):
            multiply(2, e, late1[:, (e - 2) * C:(e - 1) * C])

        nc.vector.tensor_tensor(t1[:], y[:].indirect(pos1_t[:]), gates[:, 0, :], MULT)
        for c0 in range(0, T, T // 2):
            cols = slice(c0, c0 + T // 2)
            nc.vector.tensor_tensor(
                t2[:, cols], y[:].indirect(pos2_t[:, c0 // 16:(c0 + T // 2) // 16]), gates[:, 1, cols], MULT
            )
        for c0 in range(0, T, T // 2):
            cols = slice(c0, c0 + T // 2)
            nc.vector.tensor_add(res[:, cols], t1[:, cols], t2[:, cols])
            nc.sync.dma_start(out=out[:, cols], in_=res[:, cols])
